import numpy as np
import ml_dtypes

BF16 = ml_dtypes.bfloat16


def bf(x):
    return np.asarray(x, np.float32).astype(BF16)


def f32(x):
    return np.asarray(x, np.float32)


def f64(x):
    return np.asarray(x).astype(np.float64)


def striped(idx):
    return np.tile(idx.reshape(-1, 16).T, (8, 1))


S, K, M, N, V, D = 1024, 128, 256, 256, 64, 4


def setup_inputs():
    return {"table": bf(np.random.standard_normal((K, S))), "w": bf(np.random.standard_normal((K, M)) / np.sqrt(K)), "c": f32(1.5 * np.random.standard_normal((1, N))), "b": f32(0.5 * np.random.standard_normal((M, 1))), "offs": striped(np.random.permutation(np.tile(np.arange(S), 2))[:N])}


def reference(table, w, c, b, offs):
    idx = offs[:16].T.reshape(-1)
    y = (f64(w).T @ f64(table)[:, idx]).reshape(M, V, D)
    a = np.exp(f64(c).reshape(V, D))
    a = a / a.sum(axis=1, keepdims=True)
    z = (y * a).sum(axis=2)
    return np.maximum(z + f64(b), 0.0)

@@ -1,0 +1,64 @@
+import concourse.mybir as mybir
+
+BF16, F32, U16 = mybir.dt.bfloat16, mybir.dt.float32, mybir.dt.uint16
+ALU = mybir.AluOpType
+ACT = mybir.ActivationFunctionType
+AXIS_X = mybir.AxisListType.X
+
+P = 128
+S, K, M, N = 1024, 128, 256, 256
+D = 4
+V = N // D
+BLOCKS = M // P
+
+FLOPS = 2 * K * M * N
+
+
+def tile_rows_wbag_relu_rep_kernel(tc, table, w, c, b, offs, out):
+    nc = tc.nc
+    with (
+        tc.tile_pool(name="sbuf", bufs=1) as sbuf,
+        tc.psum_pool(name="psum", bufs=1) as psum,
+    ):
+        offsets = sbuf.tile([P, N // 16], U16)
+        table_sb = sbuf.tile([K, S], BF16)
+        w_sb = sbuf.tile([K, M], BF16)
+        logits = sbuf.tile([P, V, D], F32)
+        bias = sbuf.tile([P, BLOCKS], F32)
+
+        nc.scalar.dma_start(logits[:].rearrange("p v t -> p (v t)"), c[0].partition_broadcast(P))
+        nc.sync.dma_start(table_sb[:], table)
+        nc.sync.dma_start(offsets[:], offs)
+        nc.sync.dma_start(w_sb[:], w)
+        nc.scalar.dma_start(bias[:], b.rearrange("(a p) o -> p (a o)", p=P))
+
+        top = sbuf.tile([P, V], F32)
+        shifted = sbuf.tile([P, V, D], F32)
+        expo = sbuf.tile([P, V, D], F32)
+        total = sbuf.tile([P, V], F32)
+        inverse = sbuf.tile([P, V], F32)
+        attention = sbuf.tile([P, V, D], F32)
+        nc.vector.tensor_reduce(top[:], logits[:], AXIS_X, ALU.max)
+        nc.vector.tensor_tensor(shifted[:], logits[:], top[:].unsqueeze(2).to_broadcast([P, V, D]), ALU.subtract)
+        nc.scalar.activation(expo[:], shifted[:], ACT.Exp)
+        nc.vector.tensor_reduce(total[:], expo[:], AXIS_X, ALU.add)
+        nc.vector.reciprocal(inverse[:], total[:])
+        nc.vector.tensor_tensor(attention[:], expo[:], inverse[:].unsqueeze(2).to_broadcast([P, V, D]), ALU.mult)
+
+        result = sbuf.tile([P, BLOCKS, V], F32)
+        for a in range(BLOCKS):
+            projected = psum.tile([P, V, D], F32, name=f"projected{a}")
+            weighted = sbuf.tile([P, V, D], F32, name=f"weighted{a}")
+            pooled = sbuf.tile([P, V], F32, name=f"pooled{a}")
+            nc.tensor.matmul(
+                projected[:].rearrange("p v t -> p (v t)"),
+                w_sb[:, a * P : (a + 1) * P],
+                table_sb[:].indirect(offsets[:]),
+                start=True,
+                stop=True,
+            )
+            nc.vector.tensor_tensor(weighted[:], projected[:], attention[:], ALU.mult)
+            nc.vector.tensor_reduce(pooled[:], weighted[:], AXIS_X, ALU.add)
+            nc.vector.tensor_scalar(result[:, a, :], pooled[:], bias[:, a : a + 1], 0.0, ALU.add, ALU.max)
+
+        nc.sync.dma_start(out.rearrange("(a p) v -> p a v", p=P), result[:])

@@ -1,4 +1,5 @@
 import concourse.mybir as mybir
+from concourse.masks import make_identity
 
 BF16, F32, U16 = mybir.dt.bfloat16, mybir.dt.float32, mybir.dt.uint16
 ALU = mybir.AluOpType
@@ -22,43 +23,54 @@ def tile_rows_wbag_relu_rep_kernel(tc, table, w, c, b, offs, out):
     ):
         offsets = sbuf.tile([P, N // 16], U16)
         table_sb = sbuf.tile([K, S], BF16)
-        w_sb = sbuf.tile([K, M], BF16)
-        logits = sbuf.tile([P, V, D], F32)
+        w_sb = sbuf.tile([K, P, BLOCKS], BF16)
+        logits = sbuf.tile([V, D], F32)
         bias = sbuf.tile([P, BLOCKS], F32)
 
-        nc.scalar.dma_start(logits[:].rearrange("p v t -> p (v t)"), c[0].partition_broadcast(P))
+        nc.scalar.dma_start(logits[:], c.rearrange("o (v t) -> (o v) t", t=D))
         nc.sync.dma_start(table_sb[:], table)
         nc.sync.dma_start(offsets[:], offs)
-        nc.sync.dma_start(w_sb[:], w)
-        nc.scalar.dma_start(bias[:], b.rearrange("(a p) o -> p (a o)", p=P))
+        nc.sync.dma_start(w_sb[:], w.rearrange("k (p a) -> k p a", a=BLOCKS))
+        nc.sync.dma_start(bias[:], b.rearrange("(p a) o -> p (a o)", a=BLOCKS))
 
-        top = sbuf.tile([P, V], F32)
-        shifted = sbuf.tile([P, V, D], F32)
-        expo = sbuf.tile([P, V, D], F32)
-        total = sbuf.tile([P, V], F32)
-        inverse = sbuf.tile([P, V], F32)
-        attention = sbuf.tile([P, V, D], F32)
+        identity = sbuf.tile([V, V], F32)
+        make_identity(nc, identity[:])
+
+        top = sbuf.tile([V, 1], F32)
+        shifted = sbuf.tile([V, D], F32)
+        expo = sbuf.tile([V, D], F32)
+        total = sbuf.tile([V, 1], F32)
+        inverse = sbuf.tile([V, 1], F32)
+        share = sbuf.tile([V, D], F32)
         nc.vector.tensor_reduce(top[:], logits[:], AXIS_X, ALU.max)
-        nc.vector.tensor_tensor(shifted[:], logits[:], top[:].unsqueeze(2).to_broadcast([P, V, D]), ALU.subtract)
-        nc.scalar.activation(expo[:], shifted[:], ACT.Exp)
-        nc.vector.tensor_reduce(total[:], expo[:], AXIS_X, ALU.add)
+        nc.vector.tensor_scalar(shifted[:], logits[:], top[:], None, ALU.subtract)
+        nc.scalar.activation(expo[:], shifted[:], ACT.Exp, accum_out=total[:])
         nc.vector.reciprocal(inverse[:], total[:])
-        nc.vector.tensor_tensor(attention[:], expo[:], inverse[:].unsqueeze(2).to_broadcast([P, V, D]), ALU.mult)
+        nc.vector.tensor_scalar(share[:], expo[:], inverse[:], None, ALU.mult)
 
-        result = sbuf.tile([P, BLOCKS, V], F32)
+        biased = sbuf.tile([P, BLOCKS, V, D], F32)
         for a in range(BLOCKS):
             projected = psum.tile([P, V, D], F32, name=f"projected{a}")
-            weighted = sbuf.tile([P, V, D], F32, name=f"weighted{a}")
-            pooled = sbuf.tile([P, V], F32, name=f"pooled{a}")
             nc.tensor.matmul(
                 projected[:].rearrange("p v t -> p (v t)"),
-                w_sb[:, a * P : (a + 1) * P],
+                w_sb[:, :, a],
                 table_sb[:].indirect(offsets[:]),
                 start=True,
                 stop=True,
             )
-            nc.vector.tensor_tensor(weighted[:], projected[:], attention[:], ALU.mult)
-            nc.vector.tensor_reduce(pooled[:], weighted[:], AXIS_X, ALU.add)
-            nc.vector.tensor_scalar(result[:, a, :], pooled[:], bias[:, a : a + 1], 0.0, ALU.add, ALU.max)
+            nc.scalar.activation(biased[:, a], projected[:], ACT.Identity, bias=bias[:, a : a + 1])
 
-        nc.sync.dma_start(out.rearrange("(a p) v -> p a v", p=P), result[:])
+        attention = psum.tile([P, D, V], F32)
+        for t in range(D):
+            nc.tensor.transpose(attention[:, t, :], share[:, t : t + 1].to_broadcast([V, P]), identity[:])
+
+        weighted = sbuf.tile([P, BLOCKS, V, D], F32)
+        pooled = sbuf.tile([P, BLOCKS, V], F32)
+        result = sbuf.tile([P, BLOCKS, V], F32)
+        for a in range(BLOCKS):
+            nc.vector.tensor_tensor(weighted[:, a], biased[:, a], attention[:].rearrange("p t v -> p v t"), ALU.mult)
+        for a in range(BLOCKS):
+            nc.vector.tensor_reduce(pooled[:, a], weighted[:, a], AXIS_X, ALU.add)
+        nc.vector.tensor_scalar(result[:], pooled[:], 0.0, None, ALU.max)
+
+        nc.sync.dma_start(out.rearrange("(p a) v -> p a v", a=BLOCKS), result[:])

@@ -11,6 +11,7 @@ S, K, M, N = 1024, 128, 256, 256
 D = 4
 V = N // D
 BLOCKS = M // P
+HALF = D // BLOCKS
 
 FLOPS = 2 * K * M * N
 
@@ -27,11 +28,11 @@ def tile_rows_wbag_relu_rep_kernel(tc, table, w, c, b, offs, out):
         logits = sbuf.tile([V, D], F32)
         bias = sbuf.tile([P, BLOCKS], F32)
 
-        nc.scalar.dma_start(logits[:], c.rearrange("o (v t) -> (o v) t", t=D))
+        nc.sync.dma_start(logits[:], c.rearrange("o (v t) -> (o v) t", t=D))
         nc.sync.dma_start(table_sb[:], table)
         nc.sync.dma_start(offsets[:], offs)
         nc.sync.dma_start(w_sb[:], w.rearrange("k (p a) -> k p a", a=BLOCKS))
-        nc.sync.dma_start(bias[:], b.rearrange("(p a) o -> p (a o)", a=BLOCKS))
+        nc.scalar.dma_start(bias[:], b.rearrange("(p a) o -> p (a o)", a=BLOCKS))
 
         identity = sbuf.tile([V, V], F32)
         make_identity(nc, identity[:])
@@ -41,16 +42,23 @@ def tile_rows_wbag_relu_rep_kernel(tc, table, w, c, b, offs, out):
         expo = sbuf.tile([V, D], F32)
         total = sbuf.tile([V, 1], F32)
         inverse = sbuf.tile([V, 1], F32)
-        share = sbuf.tile([V, D], F32)
         nc.vector.tensor_reduce(top[:], logits[:], AXIS_X, ALU.max)
         nc.vector.tensor_scalar(shifted[:], logits[:], top[:], None, ALU.subtract)
         nc.scalar.activation(expo[:], shifted[:], ACT.Exp, accum_out=total[:])
         nc.vector.reciprocal(inverse[:], total[:])
-        nc.vector.tensor_scalar(share[:], expo[:], inverse[:], None, ALU.mult)
 
-        biased = sbuf.tile([P, BLOCKS, V, D], F32)
+        attention = sbuf.tile([P, D, V], F32)
         for a in range(BLOCKS):
-            projected = psum.tile([P, V, D], F32, name=f"projected{a}")
+            shifted_all = psum.tile([P, HALF, V], F32, name=f"shifted_all{a}", tag=f"bank{a}")
+            for i in range(HALF):
+                t = a * HALF + i
+                nc.tensor.transpose(shifted_all[:, i, :], shifted[:, t : t + 1].to_broadcast([V, P]), identity[:])
+            nc.scalar.activation(attention[:, a * HALF : (a + 1) * HALF, :], shifted_all[:], ACT.Exp)
+
+        weighted = sbuf.tile([P, BLOCKS, V, D], F32)
+        pooled = sbuf.tile([P, BLOCKS, V], F32)
+        for a in range(BLOCKS):
+            projected = psum.tile([P, V, D], F32, name=f"projected{a}", tag=f"bank{a}")
             nc.tensor.matmul(
                 projected[:].rearrange("p v t -> p (v t)"),
                 w_sb[:, :, a],
@@ -58,19 +66,21 @@ def tile_rows_wbag_relu_rep_kernel(tc, table, w, c, b, offs, out):
                 start=True,
                 stop=True,
             )
-            nc.scalar.activation(biased[:, a], projected[:], ACT.Identity, bias=bias[:, a : a + 1])
-
-        attention = psum.tile([P, D, V], F32)
-        for t in range(D):
-            nc.tensor.transpose(attention[:, t, :], share[:, t : t + 1].to_broadcast([V, P]), identity[:])
-
-        weighted = sbuf.tile([P, BLOCKS, V, D], F32)
-        pooled = sbuf.tile([P, BLOCKS, V], F32)
-        result = sbuf.tile([P, BLOCKS, V], F32)
-        for a in range(BLOCKS):
-            nc.vector.tensor_tensor(weighted[:, a], biased[:, a], attention[:].rearrange("p t v -> p v t"), ALU.mult)
-        for a in range(BLOCKS):
+            nc.vector.scalar_tensor_tensor(
+                weighted[:, a],
+                projected[:],
+                bias[:, a : a + 1],
+                attention[:].rearrange("p t v -> p v t"),
+                ALU.add,
+                ALU.mult,
+            )
             nc.vector.tensor_reduce(pooled[:, a], weighted[:, a], AXIS_X, ALU.add)
-        nc.vector.tensor_scalar(result[:], pooled[:], 0.0, None, ALU.max)
+
+        inverse_all = psum.tile([P, V], F32, tag="bank0")
+        nc.tensor.transpose(inverse_all[:], inverse[:].to_broadcast([V, P]), identity[:])
+        result = sbuf.tile([P, BLOCKS, V], F32)
+        nc.vector.scalar_tensor_tensor(
+            result[:], pooled[:], 0.0, inverse_all[:].unsqueeze(1).to_broadcast([P, BLOCKS, V]), ALU.max, ALU.mult
+        )
 
         nc.sync.dma_start(out.rearrange("(p a) v -> p a v", a=BLOCKS), result[:])

@@ -11,7 +11,7 @@ S, K, M, N = 1024, 128, 256, 256
 D = 4
 V = N // D
 BLOCKS = M // P
-HALF = D // BLOCKS
+NEIGHBOURS_IN_BANK = (range(0, 1), range(1, D))
 
 FLOPS = 2 * K * M * N
 
@@ -48,12 +48,11 @@ def tile_rows_wbag_relu_rep_kernel(tc, table, w, c, b, offs, out):
         nc.vector.reciprocal(inverse[:], total[:])
 
         attention = sbuf.tile([P, D, V], F32)
-        for a in range(BLOCKS):
-            shifted_all = psum.tile([P, HALF, V], F32, name=f"shifted_all{a}", tag=f"bank{a}")
-            for i in range(HALF):
-                t = a * HALF + i
+        for a, neighbours in enumerate(NEIGHBOURS_IN_BANK):
+            shifted_all = psum.tile([P, len(neighbours), V], F32, name=f"shifted_all{a}", tag=f"bank{a}")
+            for i, t in enumerate(neighbours):
                 nc.tensor.transpose(shifted_all[:, i, :], shifted[:, t : t + 1].to_broadcast([V, P]), identity[:])
-            nc.scalar.activation(attention[:, a * HALF : (a + 1) * HALF, :], shifted_all[:], ACT.Exp)
+            nc.scalar.activation(attention[:, neighbours.start : neighbours.stop, :], shifted_all[:], ACT.Exp)
 
         weighted = sbuf.tile([P, BLOCKS, V, D], F32)
         pooled = sbuf.tile([P, BLOCKS, V], F32)

@@ -32,7 +32,7 @@ def tile_rows_wbag_relu_rep_kernel(tc, table, w, c, b, offs, out):
         nc.sync.dma_start(table_sb[:], table)
         nc.sync.dma_start(offsets[:], offs)
         nc.sync.dma_start(w_sb[:], w.rearrange("k (p a) -> k p a", a=BLOCKS))
-        nc.scalar.dma_start(bias[:], b.rearrange("(p a) o -> p (a o)", a=BLOCKS))
+        nc.sync.dma_start(bias[:], b.rearrange("(p a) o -> p (a o)", a=BLOCKS))
 
         identity = sbuf.tile([V, V], F32)
         make_identity(nc, identity[:])
@@ -44,7 +44,8 @@ def tile_rows_wbag_relu_rep_kernel(tc, table, w, c, b, offs, out):
         inverse = sbuf.tile([V, 1], F32)
         nc.vector.tensor_reduce(top[:], logits[:], AXIS_X, ALU.max)
         nc.vector.tensor_scalar(shifted[:], logits[:], top[:], None, ALU.subtract)
-        nc.scalar.activation(expo[:], shifted[:], ACT.Exp, accum_out=total[:])
+        nc.scalar.activation(expo[:], shifted[:], ACT.Exp)
+        nc.vector.tensor_reduce(total[:], expo[:], AXIS_X, ALU.add)
         nc.vector.reciprocal(inverse[:], total[:])
 
         attention = sbuf.tile([P, D, V], F32)

import concourse.mybir as mybir
from concourse.masks import make_identity

BF16, F32, U16 = mybir.dt.bfloat16, mybir.dt.float32, mybir.dt.uint16
ALU = mybir.AluOpType
ACT = mybir.ActivationFunctionType
AXIS_X = mybir.AxisListType.X

P = 128
S, K, M, N = 1024, 128, 256, 256
D = 4
V = N // D
BLOCKS = M // P
NEIGHBOURS_IN_BANK = (range(0, 1), range(1, D))

FLOPS = 2 * K * M * N


def tile_rows_wbag_relu_rep_kernel(tc, table, w, c, b, offs, out):
    nc = tc.nc
    with (
        tc.tile_pool(name="sbuf", bufs=1) as sbuf,
        tc.psum_pool(name="psum", bufs=1) as psum,
    ):
        offsets = sbuf.tile([P, N // 16], U16)
        table_sb = sbuf.tile([K, S], BF16)
        w_sb = sbuf.tile([K, P, BLOCKS], BF16)
        logits = sbuf.tile([V, D], F32)
        bias = sbuf.tile([P, BLOCKS], F32)

        nc.sync.dma_start(logits[:], c.rearrange("o (v t) -> (o v) t", t=D))
        nc.sync.dma_start(table_sb[:], table)
        nc.sync.dma_start(offsets[:], offs)
        nc.sync.dma_start(w_sb[:], w.rearrange("k (p a) -> k p a", a=BLOCKS))
        nc.sync.dma_start(bias[:], b.rearrange("(p a) o -> p (a o)", a=BLOCKS))

        identity = sbuf.tile([V, V], F32)
        make_identity(nc, identity[:])

        top = sbuf.tile([V, 1], F32)
        shifted = sbuf.tile([V, D], F32)
        expo = sbuf.tile([V, D], F32)
        total = sbuf.tile([V, 1], F32)
        inverse = sbuf.tile([V, 1], F32)
        nc.vector.tensor_reduce(top[:], logits[:], AXIS_X, ALU.max)
        nc.vector.tensor_scalar(shifted[:], logits[:], top[:], None, ALU.subtract)
        nc.scalar.activation(expo[:], shifted[:], ACT.Exp)
        nc.vector.tensor_reduce(total[:], expo[:], AXIS_X, ALU.add)
        nc.vector.reciprocal(inverse[:], total[:])

        attention = sbuf.tile([P, D, V], F32)
        for a, neighbours in enumerate(NEIGHBOURS_IN_BANK):
            shifted_all = psum.tile([P, len(neighbours), V], F32, name=f"shifted_all{a}", tag=f"bank{a}")
            for i, t in enumerate(neighbours):
                nc.tensor.transpose(shifted_all[:, i, :], shifted[:, t : t + 1].to_broadcast([V, P]), identity[:])
            nc.scalar.activation(attention[:, neighbours.start : neighbours.stop, :], shifted_all[:], ACT.Exp)

        weighted = sbuf.tile([P, BLOCKS, V, D], F32)
        pooled = sbuf.tile([P, BLOCKS, V], F32)
        for a in range(BLOCKS):
            projected = psum.tile([P, V, D], F32, name=f"projected{a}", tag=f"bank{a}")
            nc.tensor.matmul(
                projected[:].rearrange("p v t -> p (v t)"),
                w_sb[:, :, a],
                table_sb[:].indirect(offsets[:]),
                start=True,
                stop=True,
            )
            nc.vector.scalar_tensor_tensor(
                weighted[:, a],
                projected[:],
                bias[:, a : a + 1],
                attention[:].rearrange("p t v -> p v t"),
                ALU.add,
                ALU.mult,
            )
            nc.vector.tensor_reduce(pooled[:, a], weighted[:, a], AXIS_X, ALU.add)

        inverse_all = psum.tile([P, V], F32, tag="bank0")
        nc.tensor.transpose(inverse_all[:], inverse[:].to_broadcast([V, P]), identity[:])
        result = sbuf.tile([P, BLOCKS, V], F32)
        nc.vector.scalar_tensor_tensor(
            result[:], pooled[:], 0.0, inverse_all[:].unsqueeze(1).to_broadcast([P, BLOCKS, V]), ALU.max, ALU.mult
        )

        nc.sync.dma_start(out.rearrange("(p a) v -> p a v", a=BLOCKS), result[:])
